import numpy as np
import ml_dtypes


def mxq(x, axis, fmt="e4m3"):
    dtype, down = {"e4m3": (ml_dtypes.float8_e4m3fn, 7), "e5m2": (ml_dtypes.float8_e5m2, 14)}[fmt]
    v = np.moveaxis(np.asarray(x, np.float32).astype(ml_dtypes.bfloat16).astype(np.float64), axis, -1)
    blocks = v.reshape(v.shape[:-1] + (-1, 32))
    amax = np.abs(blocks).max(-1, keepdims=True)
    byte = np.maximum(np.where(amax > 0, np.frexp(amax)[1] - 1 + 127, 0) - down, 1)
    scale = np.exp2(byte - 127.0)
    codes = (blocks / scale).astype(np.float32).astype(dtype).astype(np.float64)
    return np.moveaxis((codes * scale).reshape(v.shape), -1, axis)


WIDE = False


def mx_kscale(k):
    if not WIDE:
        return np.ones(k)
    levels = np.array([10, -10, 5, -5, 0])
    if k % 512:
        return np.exp2(np.random.permutation(np.resize(levels, k // 32))).repeat(32)
    a = np.empty((k // 512, 16))
    for p in range(k // 512):
        a[p, :8] = np.random.permutation(np.resize(levels, 8))
        for g in range(8):
            far = levels[np.abs(levels - a[p, g]) >= 10]
            a[p, g + 8] = far[np.random.randint(len(far))]
    return np.exp2(a.ravel()).repeat(32)


BF16 = ml_dtypes.bfloat16


def bf(x):
    return np.asarray(x, np.float32).astype(BF16)


def f64(x):
    return np.asarray(x).astype(np.float64)


E2M1 = np.array([0.0, 0.5, 1.0, 1.5, 2.0, 3.0, 4.0, 6.0, -0.0, -0.5, -1.0, -1.5, -2.0, -3.0, -4.0, -6.0])


def pack_weight(w, fmt):
    k, n = w.shape
    w = f64(bf(w)).reshape(k // 32, 32, n)
    amax = np.abs(w).max(1)
    if fmt == "e4m3":
        byte = np.frexp(amax)[1] - 1 + 127 - 7
    else:
        mant, ex = np.frexp(amax / 6.0)
        byte = np.where(mant > 0.5, ex, ex - 1) + 127
    byte = np.clip(np.where(amax > 0, byte, 1), 1, 254)
    scaled = (w * np.exp2(127.0 - byte)[:, None, :]).reshape(k, n).astype(np.float32)
    by_word = np.ascontiguousarray(scaled.reshape(k // 512, 128, 4, n).transpose(0, 1, 3, 2))
    if fmt == "e4m3":
        words = by_word.astype(ml_dtypes.float8_e4m3fn).view(np.uint8)
    else:
        c = by_word.astype(ml_dtypes.float4_e2m1fn).view(np.uint8) & 0xF
        words = c[..., 0::2] | (c[..., 1::2] << 4)
    return np.ascontiguousarray(words), np.ascontiguousarray(byte.astype(np.uint8).reshape(k // 512, 16, n))


def unpack_weight(words, scales, fmt):
    g, p, n, _ = words.shape
    if fmt == "e4m3":
        vals = np.ascontiguousarray(words).view(ml_dtypes.float8_e4m3fn).astype(np.float64)
    else:
        nib = np.empty((g, p, n, 4), np.uint8)
        nib[..., 0::2] = words & 0xF
        nib[..., 1::2] = words >> 4
        vals = E2M1[nib]
    vals = vals * np.repeat(np.exp2(scales.astype(np.float64) - 127.0), 8, axis=1)[..., None]
    return vals.transpose(0, 1, 3, 2).reshape(g * 512, n)
def pack4(w):
    words, scales = pack_weight(w, "e2m1")
    return words.reshape(words.shape[0], 128, -1), scales


def unpack4(words, scales):
    return unpack_weight(words.reshape(words.shape[0], 128, -1, 2), scales, "e2m1")


def planes(Y):
    n, m = Y.shape
    b = f64(bf(Y)).reshape(n // 32, 32, m)
    amax = np.abs(b).max(1)
    byte = np.clip(np.where(amax > 0, np.frexp(amax)[1] - 1 + 127 - 7, 1), 1, 254)
    codes = (b * np.exp2(127.0 - byte)[:, None, :]).reshape(n, m).astype(np.float32).astype(ml_dtypes.float8_e4m3fn).view(np.uint8)
    words = codes.reshape(n // 512, 128, 4, m).transpose(0, 1, 3, 2)
    return np.ascontiguousarray(words), np.ascontiguousarray(byte.astype(np.uint8).reshape(n // 512, 16, m))


H, W, J = 512, 1024, 1536

def setup_inputs():
    rn = np.random.randn
    s1, s2, t = mx_kscale(H), mx_kscale(W), mx_kscale(J)
    dh = np.abs(np.arange(H)[:, None] - np.arange(H)[None, :])
    dw = np.abs(np.arange(W)[:, None] - np.arange(W)[None, :])
    rk = np.exp(0.5 * rn(H, H)) / (1.0 + dh / (H / 8.0))
    ck = np.exp(0.5 * rn(W, W)) / (1.0 + dw / (W / 8.0))
    rk = rk / np.sqrt((rk ** 2).sum(axis=1, keepdims=True))
    ck = ck / np.sqrt((ck ** 2).sum(axis=0, keepdims=True))
    u = rn(H, J)
    v = J ** -0.25 * rn(W, J)
    u_words, u_scales = pack4(u / s1[:, None])
    v_words, v_scales = pack_weight(v / s2[:, None] / t[None, :], "e4m3")
    return {"row_kernel": bf(rk * s1[None, :]), "col_kernel": bf(ck * s2[:, None]),
            "u_words": u_words, "u_scales": u_scales, "v_words": v_words, "v_scales": v_scales,
            "strength": bf(J ** -0.25 * np.exp(0.3 * rn(J)) * t), "base": bf(0.4 * J ** -0.25 * rn(J) / t),
            "static_map": bf(0.5 * rn(H, W)), "cap": bf(np.exp(0.8 * rn(W)))}

def reference(row_kernel, col_kernel, u_words, u_scales, v_words, v_scales, strength, base, static_map, cap):
    U = unpack4(u_words, u_scales)
    V = unpack_weight(v_words, v_scales, "e4m3")
    P = (mxq(f64(row_kernel), 1, "e4m3") @ U) * f64(strength)[None, :]
    Q = (V.T @ mxq(f64(col_kernel), 0, "e4m3")) + f64(base)[:, None]
    Z = mxq(P, 1, "e4m3") @ mxq(Q, 0, "e4m3")
    y = np.tanh(Z + f64(static_map)) * f64(cap)[None, :]
    Y = y.T
    words, scales = planes(Y)
    return y, words, scales

@@ -1,0 +1,397 @@
+from contextlib import ExitStack
+
+import concourse.mybir as mybir
+from concourse.masks import make_identity
+
+H, W, J = 512, 1024, 1536
+FLOPS = 2 * H * H * J + 2 * W * W * J + 2 * H * W * J
+
+F32 = mybir.dt.float32
+BF16 = mybir.dt.bfloat16
+U32 = mybir.dt.uint32
+I32 = mybir.dt.int32
+U8 = mybir.dt.uint8
+FP8X4 = mybir.dt.float8_e4m3fn_x4
+FP4X4 = mybir.dt.float4_e2m1fn_x4
+ACT = mybir.ActivationFunctionType
+ALU = mybir.AluOpType
+
+P = 128
+PACK = 4
+KP = P * PACK
+NG = J // KP
+NH = W // KP
+NA = H // P
+
+
+def tile_separable_costmap_inflation_k4_kernel(
+    tc, row_kernel, col_kernel, u_words, u_scales, v_words, v_scales, strength, base, static_map, cap,
+    out_0, out_1, out_2,
+):
+    nc = tc.nc
+    with ExitStack() as ctx:
+        sb = ctx.enter_context(tc.tile_pool(name="sb", bufs=1))
+        ps_mm = ctx.enter_context(tc.psum_pool(name="ps_mm", bufs=4))
+        ps_z = ctx.enter_context(tc.psum_pool(name="ps_z", bufs=2))
+        ps_tr = ctx.enter_context(tc.psum_pool(name="ps_tr", bufs=2))
+        ctx.enter_context(tc.manual_schedule())
+
+        def new(name, shape, dtype):
+            return sb.tile(shape, dtype, name=name, align_bytes=64)
+
+        def interleave(copy, grouped, flat, c0, c1):
+            copy(
+                out=grouped[:, c0:c1, :].rearrange("p (c i) t -> p c t i", i=4),
+                in_=flat[:, :, c0:c1].rearrange("p t (c i) -> p c t i", i=4),
+            )
+
+        def quantize(codes, scales, grouped):
+            nc.vector.quantize_mx(
+                out=codes.bitcast(FP8X4), scales=scales, in_=grouped.rearrange("p n t -> p (n t)")
+            )
+
+        def operand(name):
+            return new(name + "_codes", [P, KP], U32), new(name + "_scales", [P, KP], U8)
+
+        ident = new("ident", [P, P], F32)
+        warm = new("warm", [P, 1], F32)
+        rows_raw = new("rows_raw", [P, KP], BF16)
+        rows_f32 = new("rows_f32", [P, KP], F32)
+        consts = new("consts", [P, PACK, 2 * NG], F32)
+        r_raw = [new("r_raw%d" % b, [P, 2, H], BF16) for b in range(2)]
+        r_sorted = [new("r_sorted%d" % b, [P, 2, 2, P], F32) for b in range(2)]
+        r_grouped = new("r_grouped", [P, H, PACK], BF16)
+        r_op = operand("r")
+        u_raw = new("u_raw", [P, 2 * J], U8)
+        u_codes = new("u_codes", [P, 2 * J], U8)
+        us_raw = new("us_raw", [P, J], U8)
+        us = new("us", [P, J], U8)
+        vs_raw = new("vs_raw", [P, J], U8)
+        vs = new("vs", [P, J], U8)
+        v_raw = [new("v_raw%d" % G, [P, NH, KP], U32) for G in range(NG)]
+        v_codes = [new("v_codes%d" % G, [P, NH, KP], U32) for G in range(NG)]
+        c_raw = {(g, h): new("c_raw%d%d" % (g, h), [P, PACK, KP], BF16) for g in range(NH) for h in range(NH)}
+        c_grouped = {(g, h): new("c_grp%d%d" % (g, h), [P, KP, PACK], BF16) for g in range(NH) for h in range(NH)}
+        c_op = {(g, h): operand("c%d%d" % (g, h)) for g in range(NH) for h in range(NH)}
+        units = [(kind, G) for G in range(NG) for kind in ("p", 0)] + [(1, G) for G in range(NG)]
+        flat_tiles = [new("flat%d" % i, [P, PACK, KP], BF16) for i in range(3)]
+        grouped_tiles = [new("grp%d" % i, [P, KP, PACK], BF16) for i in range(3)]
+        flat = {u: flat_tiles[i % 3] for i, u in enumerate(units)}
+        grouped = {u: grouped_tiles[i % 3] for i, u in enumerate(units)}
+        op = {u: operand("op%s%d" % u) for u in units}
+        s_sb = new("s_sb", [P, NA, W], BF16)
+        cap_sb = new("cap_sb", [P, W], BF16)
+        cells = [(h, a) for h in range(NH) for a in range(NA)]
+        pre = {c: new("pre%d%d" % c, [P, KP], F32) for c in cells}
+        sat = {c: new("sat%d%d" % c, [P, KP], F32) for c in cells}
+        y = {c: new("y%d%d" % c, [P, KP], F32) for c in cells}
+        yb = {c: new("yb%d%d" % c, [P, KP], BF16) for c in cells}
+        yt = {c: new("yt%d%d" % c, [P, P, PACK], BF16) for c in cells}
+        y_op = [operand("yq%d" % h) for h in range(NH)]
+        z_bank = {}
+        t_bank = {}
+
+        def load_c(g, h):
+            src = col_kernel[KP * g : KP * (g + 1), KP * h : KP * (h + 1)]
+            nc.sync.dma_start(out=c_raw[g, h][:], in_=src.rearrange("(p t) w -> p t w", t=PACK))
+
+        def load_v(G):
+            src = v_words.rearrange("g p n t -> p g (n t)")[:, :, PACK * KP * G : PACK * KP * (G + 1)]
+            nc.sync.dma_start(out=v_raw[G][:].bitcast(I32), in_=src.bitcast(I32))
+
+        def sort_columns(dst, src, words):
+            nc.vector.tensor_copy(
+                out=dst.rearrange("p (G t q r) -> p G t q r", t=PACK, q=16, r=words),
+                in_=src.rearrange("p (G q t r) -> p G t q r", t=PACK, q=16, r=words),
+            )
+
+        def sort_v(G):
+            sort_columns(
+                v_codes[G][:].rearrange("p g n -> p (g n)").bitcast(I32),
+                v_raw[G][:].rearrange("p g n -> p (g n)").bitcast(I32),
+                8,
+            )
+
+        def c_inter(copy, g, h, c0, c1):
+            interleave(copy, c_grouped[g, h], c_raw[g, h], c0, c1)
+
+        def c_quant(g, h):
+            quantize(c_op[g, h][0][:], c_op[g, h][1][:], c_grouped[g, h][:])
+
+        def load_r(b):
+            src = row_kernel[2 * P * b : 2 * P * (b + 1), :]
+            nc.sync.dma_start(out=r_raw[b][:], in_=src.rearrange("(i p) k -> p i k", p=P))
+
+        def sort_r(b):
+            nc.vector.tensor_copy(
+                out=r_sorted[b][:], in_=r_raw[b][:].bitcast(F32).rearrange("p i (m u) -> p i u m", u=2)
+            )
+
+        def turn_r(b):
+            bank = ps_tr.tile([P, 2, 2, P], F32, name="tr")
+            for i in range(2):
+                for u in range(2):
+                    nc.tensor.transpose(bank[:, i, u, :], r_sorted[b][:, i, u, :], ident[:])
+            dst = r_grouped[:, 2 * P * b : 2 * P * (b + 1), :].rearrange("p n t -> p (n t)").bitcast(F32)
+            nc.scalar.copy(
+                out=dst.rearrange("p (i n u) -> p i n u", i=2, u=2), in_=bank[:].rearrange("p i u n -> p i n u")
+            )
+
+        def stage1(unit, t):
+            kind, G = unit
+            bank = ps_mm.tile([P, KP], F32, name="mm")
+            c0 = KP * G + P * t
+            if kind == "p":
+                nc.tensor.matmul_mx(
+                    out=bank[:], lhsT=u_codes[:, 2 * c0 : 2 * (c0 + P)].bitcast(FP4X4), lhsT_scale=us[:, c0 : c0 + P],
+                    rhs=r_op[0][:].bitcast(FP8X4), rhs_scale=r_op[1][:], start=True, stop=True,
+                )
+                nc.scalar.activation(out=flat[unit][:, t, :], in_=bank[:], func=ACT.Copy, scale=consts[:, t, G : G + 1])
+            else:
+                for g in range(NH):
+                    nc.tensor.matmul_mx(
+                        out=bank[:], lhsT=v_codes[G][:, g, P * t : P * (t + 1)].bitcast(FP8X4),
+                        lhsT_scale=vs[4 * g :, c0 : c0 + P],
+                        rhs=c_op[g, kind][0][:].bitcast(FP8X4), rhs_scale=c_op[g, kind][1][:],
+                        start=(g == 0), stop=(g == NH - 1),
+                    )
+                nc.scalar.activation(
+                    out=flat[unit][:, t, :], in_=bank[:], func=ACT.Identity, bias=consts[:, t, NG + G : NG + G + 1]
+                )
+
+        def stage1_all(unit):
+            for t in range(PACK):
+                stage1(unit, t)
+
+        def u_inter(unit):
+            interleave(nc.vector.tensor_copy, grouped[unit], flat[unit], 0, KP)
+
+        def u_quant(unit):
+            quantize(op[unit][0][:], op[unit][1][:], grouped[unit][:])
+
+        def z_mm(c, passes=range(NG), late=False):
+            h, a = c
+            if 0 in passes:
+                z_bank[c] = ps_mm.tile([P, KP], F32, name="mm") if late else ps_z.tile([P, KP], F32, name="z")
+            for G in passes:
+                nc.tensor.matmul_mx(
+                    out=z_bank[c][:], lhsT=op["p", G][0][:, P * a : P * (a + 1)].bitcast(FP8X4),
+                    lhsT_scale=op["p", G][1][:, P * a : P * (a + 1)],
+                    rhs=op[h, G][0][:].bitcast(FP8X4), rhs_scale=op[h, G][1][:],
+                    start=(G == 0), stop=(G == NG - 1),
+                )
+
+        def z_add(c):
+            h, a = c
+            nc.vector.tensor_tensor(out=pre[c][:], in0=z_bank[c][:], in1=s_sb[:, a, KP * h : KP * (h + 1)], op=ALU.add)
+
+        def z_tanh(c):
+            nc.scalar.activation(out=sat[c][:], in_=pre[c][:], func=ACT.Tanh)
+
+        def z_cap(c):
+            h, a = c
+            nc.vector.tensor_tensor(out=y[c][:], in0=sat[c][:], in1=cap_sb[:, KP * h : KP * (h + 1)], op=ALU.mult)
+            nc.sync.dma_start(out=out_0[P * a : P * (a + 1), KP * h : KP * (h + 1)], in_=y[c][:])
+
+        def z_round(c, copy):
+            copy(
+                out=yb[c][:].rearrange("p (u m e) -> p u m e", u=2, e=2),
+                in_=y[c][:].rearrange("p (m u e) -> p u m e", u=2, e=2),
+            )
+
+        def z_cap_round(c):
+            h, a = c
+            nc.vector.tensor_tensor(
+                out=yb[c][:].rearrange("p (u m e) -> p u m e", u=2, e=2),
+                in0=sat[c][:].rearrange("p (m u e) -> p u m e", u=2, e=2),
+                in1=cap_sb[:, KP * h : KP * (h + 1)].rearrange("p (m u e) -> p u m e", u=2, e=2),
+                op=ALU.mult,
+            )
+
+        def z_turn(c, late=False):
+            t_bank[c] = ps_mm.tile([P, 2, P], F32, name="mm") if late else ps_tr.tile([P, 2, P], F32, name="tr")
+            words = yb[c][:].bitcast(F32)
+            for u in range(2):
+                nc.tensor.transpose(t_bank[c][:, u, :], words[:, P * u : P * (u + 1)], ident[:])
+
+        def z_evac(c):
+            dst = yt[c][:].rearrange("p n t -> p (n t)").bitcast(F32)
+            nc.scalar.copy(out=dst.rearrange("p (n u) -> p n u", u=2), in_=t_bank[c][:].rearrange("p u n -> p n u"))
+
+        def z_quant(c):
+            h, a = c
+            quantize(y_op[h][0][:, P * a : P * (a + 1)], y_op[h][1][:, P * a : P * (a + 1)], yt[c][:])
+
+        def store_planes(h):
+            nc.sync.dma_start(
+                out=out_1[h].rearrange("p m t -> p (m t)").bitcast(I32), in_=y_op[h][0][:].bitcast(I32)
+            )
+            for Q in range(4):
+                queue = nc.sync if Q % 2 or h == 0 else nc.scalar
+                queue.dma_start(
+                    out=out_2[h, 4 * Q : 4 * Q + 4, :].bitcast(I32), in_=y_op[h][1][32 * Q : 32 * Q + 4, :].bitcast(I32)
+                )
+
+        nc.vector.memset(us_raw[:].bitcast(I32), 0)
+        nc.vector.memset(vs_raw[:].bitcast(I32), 0)
+        nc.vector.memset(warm[:], 0.0)
+        nc.gpsimd.dma_start(out=rows_raw[0:NG, :], in_=strength.rearrange("(G n) -> G n", G=NG))
+        nc.gpsimd.dma_start(out=rows_raw[NG : 2 * NG, :], in_=base.rearrange("(G n) -> G n", G=NG))
+        make_identity(nc, ident[:])
+        nc.gpsimd.memset(rows_f32[:], 0.0)
+
+        V, S = nc.vector.tensor_copy, nc.scalar.copy
+        load_r(0)
+        load_r(1)
+        for Q in range(4):
+            nc.scalar.dma_start(
+                out=us_raw[32 * Q : 32 * Q + 4, :].bitcast(I32), in_=u_scales[0, 4 * Q : 4 * Q + 4, :].bitcast(I32)
+            )
+        load_c(0, 0)
+        nc.sync.dma_start(out=u_raw[:].bitcast(I32), in_=u_words[0].bitcast(I32))
+        load_c(1, 0)
+        load_v(0)
+        for Q in range(4):
+            nc.sync.dma_start(
+                out=vs_raw[32 * Q : 32 * Q + 8, :].bitcast(I32), in_=v_scales[:, 4 * Q : 4 * Q + 4, :].bitcast(I32)
+            )
+        load_v(1)
+        load_c(0, 1)
+        load_v(2)
+        load_c(1, 1)
+        nc.sync.dma_start(out=s_sb[:], in_=static_map.rearrange("(a p) w -> p a w", p=P))
+        nc.sync.dma_start(out=cap_sb[:], in_=cap.partition_broadcast(P))
+
+        nc.scalar.activation(out=warm[:], in_=warm[:], func=ACT.Tanh)
+        sort_r(0)
+        sort_r(1)
+        turn_r(0)
+        turn_r(1)
+        sort_columns(us[:].bitcast(I32), us_raw[:].bitcast(I32), 2)
+        nc.vector.tensor_copy(
+            out=rows_f32[0 : 2 * NG, :].rearrange("p (t q r) -> p t q r", t=PACK, q=16),
+            in_=rows_raw[0 : 2 * NG, :].rearrange("p (q t r) -> p t q r", t=PACK, q=16),
+        )
+        const_bank = ps_z.tile([P, PACK, P], F32, name="z")
+        for t in range(PACK):
+            nc.tensor.transpose(const_bank[:, t, :], rows_f32[:, P * t : P * (t + 1)], ident[:])
+        c_inter(V, 0, 0, 0, 256)
+        sort_columns(u_codes[:].bitcast(I32), u_raw[:].bitcast(I32), 4)
+        quantize(r_op[0][:], r_op[1][:], r_grouped[:])
+        c_inter(S, 0, 0, 256, KP)
+        nc.scalar.copy(out=consts[:], in_=const_bank[:, :, 0 : 2 * NG])
+        c_inter(S, 1, 0, 384, KP)
+        c_inter(V, 1, 0, 0, 384)
+        c_quant(0, 0)
+        stage1_all(("p", 0))
+        sort_v(0)
+        c_quant(1, 0)
+        sort_columns(vs[:].bitcast(I32), vs_raw[:].bitcast(I32), 2)
+        stage1_all((0, 0))
+        sort_v(1)
+        u_inter(("p", 0))
+        c_inter(V, 0, 1, 0, KP)
+        u_quant(("p", 0))
+        stage1_all(("p", 1))
+        u_inter((0, 0))
+        c_quant(0, 1)
+        u_quant((0, 0))
+        c_inter(S, 1, 1, 384, KP)
+        stage1_all((0, 1))
+        u_inter(("p", 1))
+        sort_v(2)
+        u_quant(("p", 1))
+        c_inter(V, 1, 1, 0, 384)
+        stage1_all(("p", 2))
+        z_mm((0, 0), range(1))
+        z_mm((0, 1), range(1))
+        u_inter((0, 1))
+        c_quant(1, 1)
+        u_quant((0, 1))
+        stage1_all((0, 2))
+        u_inter(("p", 2))
+        stage1((1, 0), 0)
+        stage1((1, 0), 1)
+        z_mm((0, 0), range(1, 2))
+        z_mm((0, 1), range(1, 2))
+        u_inter((0, 2))
+        u_quant(("p", 2))
+        stage1((1, 0), 2)
+        stage1((1, 0), 3)
+        u_quant((0, 2))
+        stage1((1, 1), 0)
+        stage1((1, 1), 1)
+        z_mm((0, 0), range(2, 3))
+        z_mm((0, 1), range(2, 3))
+        u_inter((1, 0))
+        stage1((1, 1), 2)
+        z_add((0, 0))
+        u_quant((1, 0))
+        z_add((0, 1))
+        stage1((1, 1), 3)
+        z_mm((0, 2))
+        z_tanh((0, 0))
+        stage1((1, 2), 0)
+        z_mm((0, 3))
+        z_tanh((0, 1))
+        stage1((1, 2), 1)
+        u_inter((1, 1))
+        z_add((0, 2))
+        u_quant((1, 1))
+        z_add((0, 3))
+        stage1((1, 2), 2)
+        stage1((1, 2), 3)
+        z_cap((0, 0))
+        z_cap((0, 1))
+        z_mm((1, 0), range(NG - 1))
+        z_mm((1, 1), range(NG - 1))
+        z_mm((1, 2), range(NG - 1), True)
+        z_mm((1, 3), range(NG - 1), True)
+        z_tanh((0, 2))
+        z_tanh((0, 3))
+        u_inter((1, 2))
+        z_round((0, 0), S)
+        z_round((0, 1), S)
+        z_turn((0, 0))
+        z_turn((0, 1))
+        z_cap((0, 2))
+        u_quant((1, 2))
+        z_cap((0, 3))
+        for a in range(NA):
+            z_mm((1, a), range(NG - 1, NG))
+        z_round((0, 2), S)
+        z_evac((0, 0))
+        z_evac((0, 1))
+        z_round((0, 3), S)
+        z_turn((0, 2))
+        z_turn((0, 3))
+        z_add((1, 0))
+        z_add((1, 1))
+        z_evac((0, 2))
+        z_evac((0, 3))
+        z_tanh((1, 0))
+        z_add((1, 2))
+        z_tanh((1, 1))
+        z_add((1, 3))
+        for a in range(NA):
+            z_quant((0, a))
+        store_planes(0)
+        z_cap((1, 0))
+        z_tanh((1, 2))
+        z_cap((1, 1))
+        z_tanh((1, 3))
+        z_round((1, 0), S)
+        z_cap_round((1, 2))
+        z_round((1, 1), S)
+        z_cap_round((1, 3))
+        z_cap((1, 2))
+        z_cap((1, 3))
+        z_turn((1, 0))
+        z_turn((1, 2), True)
+        z_turn((1, 1))
+        z_turn((1, 3), True)
+        for a in (0, 2, 1, 3):
+            z_evac((1, a))
+        for a in (0, 2, 1, 3):
+            z_quant((1, a))
+        store_planes(1)

@@ -16,12 +16,21 @@ FP4X4 = mybir.dt.float4_e2m1fn_x4
 ACT = mybir.ActivationFunctionType
 ALU = mybir.AluOpType
 
-P = 128
-PACK = 4
-KP = P * PACK
-NG = J // KP
-NH = W // KP
-NA = H // P
+PARTS = 128
+SLOTS = 4
+PASS = PARTS * SLOTS
+BLOCKS = 16
+RUN = 8
+QUADS = 4
+OBJ_GROUPS = J // PASS
+COL_GROUPS = W // PASS
+ROW_TILES = H // PARTS
+ROW_HALF = H // 2
+ROTATE = 3
+
+SCALAR_FROM_C00 = 320
+SCALAR_FROM_C10 = 384
+SCALAR_ROUNDS = 2
 
 
 def tile_separable_costmap_inflation_k4_kernel(
@@ -29,6 +38,7 @@ def tile_separable_costmap_inflation_k4_kernel(
     out_0, out_1, out_2,
 ):
     nc = tc.nc
+    on_vector, on_scalar = nc.vector.tensor_copy, nc.scalar.copy
     with ExitStack() as ctx:
         sb = ctx.enter_context(tc.tile_pool(name="sb", bufs=1))
         ps_mm = ctx.enter_context(tc.psum_pool(name="ps_mm", bufs=4))
@@ -39,359 +49,378 @@ def tile_separable_costmap_inflation_k4_kernel(
         def new(name, shape, dtype):
             return sb.tile(shape, dtype, name=name, align_bytes=64)
 
-        def interleave(copy, grouped, flat, c0, c1):
-            copy(
-                out=grouped[:, c0:c1, :].rearrange("p (c i) t -> p c t i", i=4),
-                in_=flat[:, :, c0:c1].rearrange("p t (c i) -> p c t i", i=4),
-            )
+        def mx_pair(name, width):
+            return new(name + "_codes", [PARTS, width], U32), new(name + "_scales", [PARTS, width], U8)
 
-        def quantize(codes, scales, grouped):
-            nc.vector.quantize_mx(
-                out=codes.bitcast(FP8X4), scales=scales, in_=grouped.rearrange("p n t -> p (n t)")
-            )
+        ident = new("ident", [PARTS, PARTS], F32)
+        warm = new("warm", [PARTS, 1], F32)
+        vec_raw = new("vec_raw", [PARTS, PASS], BF16)
+        vec_sorted = new("vec_sorted", [PARTS, PASS], F32)
+        vec = new("vec", [PARTS, SLOTS, 2 * OBJ_GROUPS], F32)
+        r_raw = [new("r_raw%d" % b, [PARTS, 2, H], BF16) for b in range(2)]
+        r_sorted = new("r_sorted", [PARTS, 2, 2, PARTS], F32)
+        r_words = [new("r_words%d" % b, [PARTS, ROW_HALF, SLOTS], BF16) for b in range(2)]
+        r_mx = [mx_pair("r%d" % b, ROW_HALF) for b in range(2)]
+        u_raw = new("u_raw", [PARTS, 2 * J], U8)
+        u_codes = new("u_codes", [PARTS, 2 * J], U8)
+        u_sc_raw = new("u_sc_raw", [PARTS, J], U8)
+        u_sc = new("u_sc", [PARTS, J], U8)
+        v_raw = [new("v_raw%d" % G, [PARTS, COL_GROUPS, PASS], U32) for G in range(OBJ_GROUPS)]
+        v_codes = [new("v_codes%d" % G, [PARTS, COL_GROUPS, PASS], U32) for G in range(OBJ_GROUPS)]
+        v_sc_raw = new("v_sc_raw", [PARTS, J], U8)
+        v_sc = new("v_sc", [PARTS, J], U8)
+        c_parts = [(g, half) for g in range(COL_GROUPS) for half in range(COL_GROUPS)]
+        c_raw = {c: new("c_raw%d%d" % c, [PARTS, SLOTS, PASS], BF16) for c in c_parts}
+        c_words = {c: new("c_words%d%d" % c, [PARTS, PASS, SLOTS], BF16) for c in c_parts}
+        c_mx = {c: mx_pair("c%d%d" % c, PASS) for c in c_parts}
 
-        def operand(name):
-            return new(name + "_codes", [P, KP], U32), new(name + "_scales", [P, KP], U8)
+        by_slot, by_word, unit_mx = {}, {}, {}
+        for kind, width, word_tiles in (("q", PASS, 2), ("p", ROW_HALF, ROTATE)):
+            slot_ring = [new("%s_slot%d" % (kind, i), [PARTS, SLOTS, width], BF16) for i in range(ROTATE)]
+            word_ring = [new("%s_word%d" % (kind, i), [PARTS, width, SLOTS], BF16) for i in range(word_tiles)]
+            for i in range(2 * OBJ_GROUPS):
+                unit = (kind, i // OBJ_GROUPS, i % OBJ_GROUPS)
+                by_slot[unit] = slot_ring[i % ROTATE]
+                by_word[unit] = word_ring[i % word_tiles]
+                unit_mx[unit] = mx_pair("%s%d%d" % unit, width)
 
-        ident = new("ident", [P, P], F32)
-        warm = new("warm", [P, 1], F32)
-        rows_raw = new("rows_raw", [P, KP], BF16)
-        rows_f32 = new("rows_f32", [P, KP], F32)
-        consts = new("consts", [P, PACK, 2 * NG], F32)
-        r_raw = [new("r_raw%d" % b, [P, 2, H], BF16) for b in range(2)]
-        r_sorted = [new("r_sorted%d" % b, [P, 2, 2, P], F32) for b in range(2)]
-        r_grouped = new("r_grouped", [P, H, PACK], BF16)
-        r_op = operand("r")
-        u_raw = new("u_raw", [P, 2 * J], U8)
-        u_codes = new("u_codes", [P, 2 * J], U8)
-        us_raw = new("us_raw", [P, J], U8)
-        us = new("us", [P, J], U8)
-        vs_raw = new("vs_raw", [P, J], U8)
-        vs = new("vs", [P, J], U8)
-        v_raw = [new("v_raw%d" % G, [P, NH, KP], U32) for G in range(NG)]
-        v_codes = [new("v_codes%d" % G, [P, NH, KP], U32) for G in range(NG)]
-        c_raw = {(g, h): new("c_raw%d%d" % (g, h), [P, PACK, KP], BF16) for g in range(NH) for h in range(NH)}
-        c_grouped = {(g, h): new("c_grp%d%d" % (g, h), [P, KP, PACK], BF16) for g in range(NH) for h in range(NH)}
-        c_op = {(g, h): operand("c%d%d" % (g, h)) for g in range(NH) for h in range(NH)}
-        units = [(kind, G) for G in range(NG) for kind in ("p", 0)] + [(1, G) for G in range(NG)]
-        flat_tiles = [new("flat%d" % i, [P, PACK, KP], BF16) for i in range(3)]
-        grouped_tiles = [new("grp%d" % i, [P, KP, PACK], BF16) for i in range(3)]
-        flat = {u: flat_tiles[i % 3] for i, u in enumerate(units)}
-        grouped = {u: grouped_tiles[i % 3] for i, u in enumerate(units)}
-        op = {u: operand("op%s%d" % u) for u in units}
-        s_sb = new("s_sb", [P, NA, W], BF16)
-        cap_sb = new("cap_sb", [P, W], BF16)
-        cells = [(h, a) for h in range(NH) for a in range(NA)]
-        pre = {c: new("pre%d%d" % c, [P, KP], F32) for c in cells}
-        sat = {c: new("sat%d%d" % c, [P, KP], F32) for c in cells}
-        y = {c: new("y%d%d" % c, [P, KP], F32) for c in cells}
-        yb = {c: new("yb%d%d" % c, [P, KP], BF16) for c in cells}
-        yt = {c: new("yt%d%d" % c, [P, P, PACK], BF16) for c in cells}
-        y_op = [operand("yq%d" % h) for h in range(NH)]
-        z_bank = {}
-        t_bank = {}
+        static_sb = new("static_sb", [PARTS, ROW_TILES, W], BF16)
+        cap_sb = new("cap_sb", [PARTS, W], BF16)
+        cells = [(half, a) for half in range(COL_GROUPS) for a in range(ROW_TILES)]
+        pre = {c: new("pre%d%d" % c, [PARTS, PASS], F32) for c in cells}
+        sat = {c: new("sat%d%d" % c, [PARTS, PASS], F32) for c in cells}
+        y = {c: new("y%d%d" % c, [PARTS, PASS], F32) for c in cells}
+        y_bf = {c: new("y_bf%d%d" % c, [PARTS, PASS], BF16) for c in cells}
+        y_words = {c: new("y_words%d%d" % c, [PARTS, PARTS, SLOTS], BF16) for c in cells}
+        y_codes = [new("y_codes%d" % half, [PARTS, H], U32) for half in range(COL_GROUPS)]
+        y_scales = new("y_scales", [PARTS, H], U8)
+        z_bank, turned = {}, {}
 
-        def load_c(g, h):
-            src = col_kernel[KP * g : KP * (g + 1), KP * h : KP * (h + 1)]
-            nc.sync.dma_start(out=c_raw[g, h][:], in_=src.rearrange("(p t) w -> p t w", t=PACK))
+        def load_r(b):
+            src = row_kernel[ROW_HALF * b : ROW_HALF * (b + 1), :]
+            nc.sync.dma_start(out=r_raw[b][:], in_=src.rearrange("(i p) k -> p i k", p=PARTS))
+
+        def load_c(g, half):
+            src = col_kernel[PASS * g : PASS * (g + 1), PASS * half : PASS * (half + 1)]
+            nc.sync.dma_start(out=c_raw[g, half][:], in_=src.rearrange("(p t) w -> p t w", t=SLOTS))
 
         def load_v(G):
-            src = v_words.rearrange("g p n t -> p g (n t)")[:, :, PACK * KP * G : PACK * KP * (G + 1)]
+            src = v_words.rearrange("g p n t -> p g (n t)")[:, :, SLOTS * PASS * G : SLOTS * PASS * (G + 1)]
             nc.sync.dma_start(out=v_raw[G][:].bitcast(I32), in_=src.bitcast(I32))
 
-        def sort_columns(dst, src, words):
+        def load_scales(queue, dst, src, quads):
+            rows = 4 * src.shape[0]
+            for Q in quads:
+                queue.dma_start(
+                    out=dst[32 * Q : 32 * Q + rows, :].bitcast(I32), in_=src[:, 4 * Q : 4 * Q + 4, :].bitcast(I32)
+                )
+
+        def sort_objects(dst, src, run_words):
             nc.vector.tensor_copy(
-                out=dst.rearrange("p (G t q r) -> p G t q r", t=PACK, q=16, r=words),
-                in_=src.rearrange("p (G q t r) -> p G t q r", t=PACK, q=16, r=words),
+                out=dst.bitcast(I32).rearrange("p (G t q r) -> p G t q r", t=SLOTS, q=BLOCKS, r=run_words),
+                in_=src.bitcast(I32).rearrange("p (G q t r) -> p G t q r", t=SLOTS, q=BLOCKS, r=run_words),
             )
 
         def sort_v(G):
-            sort_columns(
-                v_codes[G][:].rearrange("p g n -> p (g n)").bitcast(I32),
-                v_raw[G][:].rearrange("p g n -> p (g n)").bitcast(I32),
-                8,
+            sort_objects(v_codes[G][:].rearrange("p g n -> p (g n)"), v_raw[G][:].rearrange("p g n -> p (g n)"), RUN)
+
+        def interleave(copy, words, slots, c0, c1):
+            copy(
+                out=words[:, c0:c1, :].rearrange("p (c i) t -> p c t i", i=4),
+                in_=slots[:, :, c0:c1].rearrange("p t (c i) -> p c t i", i=4),
             )
 
-        def c_inter(copy, g, h, c0, c1):
-            interleave(copy, c_grouped[g, h], c_raw[g, h], c0, c1)
+        def quantize(codes, scales, words):
+            nc.vector.quantize_mx(out=codes.bitcast(FP8X4), scales=scales, in_=words.rearrange("p n t -> p (n t)"))
 
-        def c_quant(g, h):
-            quantize(c_op[g, h][0][:], c_op[g, h][1][:], c_grouped[g, h][:])
+        def c_interleave(copy, g, half, c0, c1):
+            interleave(copy, c_words[g, half], c_raw[g, half], c0, c1)
 
-        def load_r(b):
-            src = row_kernel[2 * P * b : 2 * P * (b + 1), :]
-            nc.sync.dma_start(out=r_raw[b][:], in_=src.rearrange("(i p) k -> p i k", p=P))
+        def c_quantize(g, half):
+            quantize(c_mx[g, half][0][:], c_mx[g, half][1][:], c_words[g, half][:])
 
-        def sort_r(b):
-            nc.vector.tensor_copy(
-                out=r_sorted[b][:], in_=r_raw[b][:].bitcast(F32).rearrange("p i (m u) -> p i u m", u=2)
-            )
-
-        def turn_r(b):
-            bank = ps_tr.tile([P, 2, 2, P], F32, name="tr")
+        def turn_r(b, pairs_of):
+            bank = ps_tr.tile([PARTS, 2, 2, PARTS], F32, name="tr")
             for i in range(2):
                 for u in range(2):
-                    nc.tensor.transpose(bank[:, i, u, :], r_sorted[b][:, i, u, :], ident[:])
-            dst = r_grouped[:, 2 * P * b : 2 * P * (b + 1), :].rearrange("p n t -> p (n t)").bitcast(F32)
+                    nc.tensor.transpose(bank[:, i, u, :], pairs_of(i, u), ident[:])
+            dst = r_words[b][:].rearrange("p n t -> p (n t)").bitcast(F32)
             nc.scalar.copy(
                 out=dst.rearrange("p (i n u) -> p i n u", i=2, u=2), in_=bank[:].rearrange("p i u n -> p i n u")
             )
 
-        def stage1(unit, t):
-            kind, G = unit
-            bank = ps_mm.tile([P, KP], F32, name="mm")
-            c0 = KP * G + P * t
-            if kind == "p":
-                nc.tensor.matmul_mx(
-                    out=bank[:], lhsT=u_codes[:, 2 * c0 : 2 * (c0 + P)].bitcast(FP4X4), lhsT_scale=us[:, c0 : c0 + P],
-                    rhs=r_op[0][:].bitcast(FP8X4), rhs_scale=r_op[1][:], start=True, stop=True,
-                )
-                nc.scalar.activation(out=flat[unit][:, t, :], in_=bank[:], func=ACT.Copy, scale=consts[:, t, G : G + 1])
-            else:
-                for g in range(NH):
+        def r_quantize(b):
+            quantize(r_mx[b][0][:], r_mx[b][1][:], r_words[b][:])
+
+        def p_unit(b, G):
+            for t0 in range(0, SLOTS, 2):
+                bank = ps_mm.tile([PARTS, 2, ROW_HALF], F32, name="mm")
+                for e in range(2):
+                    c0 = PASS * G + PARTS * (t0 + e)
                     nc.tensor.matmul_mx(
-                        out=bank[:], lhsT=v_codes[G][:, g, P * t : P * (t + 1)].bitcast(FP8X4),
-                        lhsT_scale=vs[4 * g :, c0 : c0 + P],
-                        rhs=c_op[g, kind][0][:].bitcast(FP8X4), rhs_scale=c_op[g, kind][1][:],
-                        start=(g == 0), stop=(g == NH - 1),
+                        out=bank[:, e, :],
+                        lhsT=u_codes[:, 2 * c0 : 2 * (c0 + PARTS)].bitcast(FP4X4),
+                        lhsT_scale=u_sc[:, c0 : c0 + PARTS],
+                        rhs=r_mx[b][0][:].bitcast(FP8X4),
+                        rhs_scale=r_mx[b][1][:],
+                        start=True,
+                        stop=True,
                     )
-                nc.scalar.activation(
-                    out=flat[unit][:, t, :], in_=bank[:], func=ACT.Identity, bias=consts[:, t, NG + G : NG + G + 1]
-                )
+                for e in range(2):
+                    nc.scalar.activation(
+                        out=by_slot["p", b, G][:, t0 + e, :], in_=bank[:, e, :], func=ACT.Copy,
+                        scale=vec[:, t0 + e, G : G + 1],
+                    )
 
-        def stage1_all(unit):
-            for t in range(PACK):
-                stage1(unit, t)
-
-        def u_inter(unit):
-            interleave(nc.vector.tensor_copy, grouped[unit], flat[unit], 0, KP)
-
-        def u_quant(unit):
-            quantize(op[unit][0][:], op[unit][1][:], grouped[unit][:])
-
-        def z_mm(c, passes=range(NG), late=False):
-            h, a = c
-            if 0 in passes:
-                z_bank[c] = ps_mm.tile([P, KP], F32, name="mm") if late else ps_z.tile([P, KP], F32, name="z")
-            for G in passes:
+        def q_slot(half, G, t):
+            bank = ps_mm.tile([PARTS, PASS], F32, name="mm")
+            c0 = PASS * G + PARTS * t
+            for g in range(COL_GROUPS):
                 nc.tensor.matmul_mx(
-                    out=z_bank[c][:], lhsT=op["p", G][0][:, P * a : P * (a + 1)].bitcast(FP8X4),
-                    lhsT_scale=op["p", G][1][:, P * a : P * (a + 1)],
-                    rhs=op[h, G][0][:].bitcast(FP8X4), rhs_scale=op[h, G][1][:],
-                    start=(G == 0), stop=(G == NG - 1),
+                    out=bank[:],
+                    lhsT=v_codes[G][:, g, PARTS * t : PARTS * (t + 1)].bitcast(FP8X4),
+                    lhsT_scale=v_sc[4 * g :, c0 : c0 + PARTS],
+                    rhs=c_mx[g, half][0][:].bitcast(FP8X4),
+                    rhs_scale=c_mx[g, half][1][:],
+                    start=(g == 0),
+                    stop=(g == COL_GROUPS - 1),
                 )
+            nc.scalar.activation(
+                out=by_slot["q", half, G][:, t, :], in_=bank[:], func=ACT.Identity,
+                bias=vec[:, t, OBJ_GROUPS + G : OBJ_GROUPS + G + 1],
+            )
+
+        def unit_interleave(unit, copy=on_vector):
+            interleave(copy, by_word[unit], by_slot[unit], 0, by_word[unit].shape[1])
+
+        def unit_quantize(unit):
+            quantize(unit_mx[unit][0][:], unit_mx[unit][1][:], by_word[unit][:])
+
+        def z_pass(c, G):
+            half, a = c
+            if G == 0:
+                spare = half == 1 and a >= 2
+                z_bank[c] = (ps_mm if spare else ps_z).tile([PARTS, PASS], F32, name="mm" if spare else "z")
+            p_codes, p_scales = unit_mx["p", a // 2, G]
+            q_codes, q_scales = unit_mx["q", half, G]
+            rows = slice(PARTS * (a % 2), PARTS * (a % 2 + 1))
+            nc.tensor.matmul_mx(
+                out=z_bank[c][:],
+                lhsT=p_codes[:, rows].bitcast(FP8X4),
+                lhsT_scale=p_scales[:, rows],
+                rhs=q_codes[:].bitcast(FP8X4),
+                rhs_scale=q_scales[:],
+                start=(G == 0),
+                stop=(G == OBJ_GROUPS - 1),
+            )
 
         def z_add(c):
-            h, a = c
-            nc.vector.tensor_tensor(out=pre[c][:], in0=z_bank[c][:], in1=s_sb[:, a, KP * h : KP * (h + 1)], op=ALU.add)
+            half, a = c
+            nc.vector.tensor_tensor(
+                out=pre[c][:], in0=z_bank[c][:], in1=static_sb[:, a, PASS * half : PASS * (half + 1)], op=ALU.add
+            )
 
         def z_tanh(c):
             nc.scalar.activation(out=sat[c][:], in_=pre[c][:], func=ACT.Tanh)
 
         def z_cap(c):
-            h, a = c
-            nc.vector.tensor_tensor(out=y[c][:], in0=sat[c][:], in1=cap_sb[:, KP * h : KP * (h + 1)], op=ALU.mult)
-            nc.sync.dma_start(out=out_0[P * a : P * (a + 1), KP * h : KP * (h + 1)], in_=y[c][:])
+            half, a = c
+            cols = slice(PASS * half, PASS * (half + 1))
+            nc.vector.tensor_tensor(out=y[c][:], in0=sat[c][:], in1=cap_sb[:, cols], op=ALU.mult)
+            nc.sync.dma_start(out=out_0[PARTS * a : PARTS * (a + 1), cols], in_=y[c][:])
 
-        def z_round(c, copy):
+        def y_round(c, copy):
             copy(
-                out=yb[c][:].rearrange("p (u m e) -> p u m e", u=2, e=2),
+                out=y_bf[c][:].rearrange("p (u m e) -> p u m e", u=2, e=2),
                 in_=y[c][:].rearrange("p (m u e) -> p u m e", u=2, e=2),
             )
 
-        def z_cap_round(c):
-            h, a = c
-            nc.vector.tensor_tensor(
-                out=yb[c][:].rearrange("p (u m e) -> p u m e", u=2, e=2),
-                in0=sat[c][:].rearrange("p (m u e) -> p u m e", u=2, e=2),
-                in1=cap_sb[:, KP * h : KP * (h + 1)].rearrange("p (m u e) -> p u m e", u=2, e=2),
-                op=ALU.mult,
-            )
-
-        def z_turn(c, late=False):
-            t_bank[c] = ps_mm.tile([P, 2, P], F32, name="mm") if late else ps_tr.tile([P, 2, P], F32, name="tr")
-            words = yb[c][:].bitcast(F32)
+        def y_turn(c):
+            half, a = c
+            spare = half == 1 and a >= 2
+            turned[c] = (ps_mm if spare else ps_tr).tile([PARTS, 2, PARTS], F32, name="mm" if spare else "tr")
+            pairs = y_bf[c][:].bitcast(F32)
             for u in range(2):
-                nc.tensor.transpose(t_bank[c][:, u, :], words[:, P * u : P * (u + 1)], ident[:])
+                nc.tensor.transpose(turned[c][:, u, :], pairs[:, PARTS * u : PARTS * (u + 1)], ident[:])
 
-        def z_evac(c):
-            dst = yt[c][:].rearrange("p n t -> p (n t)").bitcast(F32)
-            nc.scalar.copy(out=dst.rearrange("p (n u) -> p n u", u=2), in_=t_bank[c][:].rearrange("p u n -> p n u"))
+        def y_empty(c):
+            dst = y_words[c][:].rearrange("p n t -> p (n t)").bitcast(F32)
+            nc.scalar.copy(out=dst.rearrange("p (n u) -> p n u", u=2), in_=turned[c][:].rearrange("p u n -> p n u"))
 
-        def z_quant(c):
-            h, a = c
-            quantize(y_op[h][0][:, P * a : P * (a + 1)], y_op[h][1][:, P * a : P * (a + 1)], yt[c][:])
+        def y_quantize(c):
+            half, a = c
+            rows = slice(PARTS * a, PARTS * (a + 1))
+            quantize(y_codes[half][:, rows], y_scales[4 * half :, rows], y_words[c][:])
 
-        def store_planes(h):
+        def store_codes(half, m0, m1):
             nc.sync.dma_start(
-                out=out_1[h].rearrange("p m t -> p (m t)").bitcast(I32), in_=y_op[h][0][:].bitcast(I32)
+                out=out_1[half, :, m0:m1, :].rearrange("p m t -> p (m t)").bitcast(I32),
+                in_=y_codes[half][:, m0:m1].bitcast(I32),
             )
-            for Q in range(4):
-                queue = nc.sync if Q % 2 or h == 0 else nc.scalar
-                queue.dma_start(
-                    out=out_2[h, 4 * Q : 4 * Q + 4, :].bitcast(I32), in_=y_op[h][1][32 * Q : 32 * Q + 4, :].bitcast(I32)
-                )
 
-        nc.vector.memset(us_raw[:].bitcast(I32), 0)
-        nc.vector.memset(vs_raw[:].bitcast(I32), 0)
+
+        nc.vector.memset(u_sc_raw[:].bitcast(I32), 0)
         nc.vector.memset(warm[:], 0.0)
-        nc.gpsimd.dma_start(out=rows_raw[0:NG, :], in_=strength.rearrange("(G n) -> G n", G=NG))
-        nc.gpsimd.dma_start(out=rows_raw[NG : 2 * NG, :], in_=base.rearrange("(G n) -> G n", G=NG))
+        nc.vector.memset(v_sc_raw[:].bitcast(I32), 0)
+        nc.vector.memset(vec_sorted[:], 0.0)
         make_identity(nc, ident[:])
-        nc.gpsimd.memset(rows_f32[:], 0.0)
 
-        V, S = nc.vector.tensor_copy, nc.scalar.copy
         load_r(0)
-        load_r(1)
-        for Q in range(4):
-            nc.scalar.dma_start(
-                out=us_raw[32 * Q : 32 * Q + 4, :].bitcast(I32), in_=u_scales[0, 4 * Q : 4 * Q + 4, :].bitcast(I32)
-            )
-        load_c(0, 0)
         nc.sync.dma_start(out=u_raw[:].bitcast(I32), in_=u_words[0].bitcast(I32))
+        load_c(0, 0)
+        for i, vector in enumerate((strength, base)):
+            nc.scalar.dma_start(
+                out=vec_raw[OBJ_GROUPS * i : OBJ_GROUPS * (i + 1), :], in_=vector.rearrange("(G n) -> G n", G=OBJ_GROUPS)
+            )
+        load_scales(nc.scalar, u_sc_raw, u_scales, range(QUADS - 1))
+        load_scales(nc.sync, u_sc_raw, u_scales, range(QUADS - 1, QUADS))
         load_c(1, 0)
         load_v(0)
-        for Q in range(4):
-            nc.sync.dma_start(
-                out=vs_raw[32 * Q : 32 * Q + 8, :].bitcast(I32), in_=v_scales[:, 4 * Q : 4 * Q + 4, :].bitcast(I32)
-            )
+        load_scales(nc.sync, v_sc_raw, v_scales, range(QUADS))
+        load_r(1)
         load_v(1)
         load_c(0, 1)
         load_v(2)
         load_c(1, 1)
-        nc.sync.dma_start(out=s_sb[:], in_=static_map.rearrange("(a p) w -> p a w", p=P))
-        nc.sync.dma_start(out=cap_sb[:], in_=cap.partition_broadcast(P))
+        nc.sync.dma_start(out=static_sb[:], in_=static_map.rearrange("(a p) w -> p a w", p=PARTS))
+        nc.sync.dma_start(out=cap_sb[:], in_=cap.partition_broadcast(PARTS))
 
         nc.scalar.activation(out=warm[:], in_=warm[:], func=ACT.Tanh)
-        sort_r(0)
-        sort_r(1)
-        turn_r(0)
-        turn_r(1)
-        sort_columns(us[:].bitcast(I32), us_raw[:].bitcast(I32), 2)
+
         nc.vector.tensor_copy(
-            out=rows_f32[0 : 2 * NG, :].rearrange("p (t q r) -> p t q r", t=PACK, q=16),
-            in_=rows_raw[0 : 2 * NG, :].rearrange("p (q t r) -> p t q r", t=PACK, q=16),
+            out=r_sorted[:], in_=r_raw[0][:].bitcast(F32).rearrange("p i (m u) -> p i u m", u=2)
         )
-        const_bank = ps_z.tile([P, PACK, P], F32, name="z")
-        for t in range(PACK):
-            nc.tensor.transpose(const_bank[:, t, :], rows_f32[:, P * t : P * (t + 1)], ident[:])
-        c_inter(V, 0, 0, 0, 256)
-        sort_columns(u_codes[:].bitcast(I32), u_raw[:].bitcast(I32), 4)
-        quantize(r_op[0][:], r_op[1][:], r_grouped[:])
-        c_inter(S, 0, 0, 256, KP)
-        nc.scalar.copy(out=consts[:], in_=const_bank[:, :, 0 : 2 * NG])
-        c_inter(S, 1, 0, 384, KP)
-        c_inter(V, 1, 0, 0, 384)
-        c_quant(0, 0)
-        stage1_all(("p", 0))
+        turn_r(0, lambda i, u: r_sorted[:, i, u, :])
+        sort_objects(u_codes[:], u_raw[:], RUN // 2)
+        nc.vector.tensor_copy(
+            out=vec_sorted[0 : 2 * OBJ_GROUPS, :].rearrange("p (t q r) -> p t q r", t=SLOTS, q=BLOCKS),
+            in_=vec_raw[0 : 2 * OBJ_GROUPS, :].rearrange("p (q t r) -> p t q r", t=SLOTS, q=BLOCKS),
+        )
+        c_interleave(on_vector, 0, 0, 0, PARTS)
+        r_quantize(0)
+        sort_objects(u_sc[:], u_sc_raw[:], RUN // 4)
+        c_interleave(on_scalar, 0, 0, SCALAR_FROM_C00, PASS)
+        vec_bank = ps_z.tile([PARTS, SLOTS, PARTS], F32, name="z")
+        for t in range(SLOTS):
+            nc.tensor.transpose(vec_bank[:, t, :], vec_sorted[:, PARTS * t : PARTS * (t + 1)], ident[:])
+        nc.scalar.copy(out=vec[:], in_=vec_bank[:, :, 0 : 2 * OBJ_GROUPS])
+        c_interleave(on_vector, 0, 0, PARTS, SCALAR_FROM_C00)
+        c_interleave(on_scalar, 1, 0, SCALAR_FROM_C10, PASS)
+
+        for G in range(OBJ_GROUPS):
+            p_unit(0, G)
+        c_interleave(on_vector, 1, 0, 0, SCALAR_FROM_C10)
+        c_quantize(0, 0)
         sort_v(0)
-        c_quant(1, 0)
-        sort_columns(vs[:].bitcast(I32), vs_raw[:].bitcast(I32), 2)
-        stage1_all((0, 0))
-        sort_v(1)
-        u_inter(("p", 0))
-        c_inter(V, 0, 1, 0, KP)
-        u_quant(("p", 0))
-        stage1_all(("p", 1))
-        u_inter((0, 0))
-        c_quant(0, 1)
-        u_quant((0, 0))
-        c_inter(S, 1, 1, 384, KP)
-        stage1_all((0, 1))
-        u_inter(("p", 1))
-        sort_v(2)
-        u_quant(("p", 1))
-        c_inter(V, 1, 1, 0, 384)
-        stage1_all(("p", 2))
-        z_mm((0, 0), range(1))
-        z_mm((0, 1), range(1))
-        u_inter((0, 1))
-        c_quant(1, 1)
-        u_quant((0, 1))
-        stage1_all((0, 2))
-        u_inter(("p", 2))
-        stage1((1, 0), 0)
-        stage1((1, 0), 1)
-        z_mm((0, 0), range(1, 2))
-        z_mm((0, 1), range(1, 2))
-        u_inter((0, 2))
-        u_quant(("p", 2))
-        stage1((1, 0), 2)
-        stage1((1, 0), 3)
-        u_quant((0, 2))
-        stage1((1, 1), 0)
-        stage1((1, 1), 1)
-        z_mm((0, 0), range(2, 3))
-        z_mm((0, 1), range(2, 3))
-        u_inter((1, 0))
-        stage1((1, 1), 2)
-        z_add((0, 0))
-        u_quant((1, 0))
-        z_add((0, 1))
-        stage1((1, 1), 3)
-        z_mm((0, 2))
-        z_tanh((0, 0))
-        stage1((1, 2), 0)
-        z_mm((0, 3))
-        z_tanh((0, 1))
-        stage1((1, 2), 1)
-        u_inter((1, 1))
+        c_quantize(1, 0)
+        sort_objects(v_sc[:], v_sc_raw[:], RUN // 4)
+
+        between = [
+            [lambda: sort_v(1)],
+            [lambda: c_interleave(on_vector, 0, 1, 0, PASS), lambda: sort_v(2)],
+            [lambda: r_quantize(1)],
+        ]
+        for G in range(OBJ_GROUPS):
+            for t in range(SLOTS):
+                q_slot(0, G, t)
+                if (G, t) == (0, 1):
+                    turn_r(1, lambda i, u: r_raw[1][:, i, :].bitcast(F32)[:, u : 2 * PARTS : 2])
+            unit_interleave(("p", 0, G))
+            for work in between[G]:
+                work()
+            unit_quantize(("p", 0, G))
+
+        between = [
+            lambda: c_quantize(0, 1),
+            lambda: c_interleave(on_vector, 1, 1, 0, PASS),
+            lambda: c_quantize(1, 1),
+        ]
+        for G in range(OBJ_GROUPS):
+            p_unit(1, G)
+            unit_interleave(("q", 0, G))
+            between[G]()
+            unit_quantize(("q", 0, G))
+        last = OBJ_GROUPS - 1
+        unit_interleave(("p", 1, last), on_scalar)
+
+        for a in range(2):
+            for G in range(last):
+                z_pass((0, a), G)
+        for t in range(SLOTS - 1):
+            q_slot(1, 0, t)
+        for a in range(2):
+            z_pass((0, a), last)
+        q_slot(1, 0, SLOTS - 1)
+        for G in range(last):
+            unit_interleave(("p", 1, G))
+        for G in range(OBJ_GROUPS):
+            unit_quantize(("p", 1, G))
+        for a in range(2):
+            z_add((0, a))
+
+        for t in range(2):
+            q_slot(1, 1, t)
+        for a in range(2):
+            for G in range(OBJ_GROUPS):
+                z_pass((0, 2 + a), G)
+            z_tanh((0, a))
+            q_slot(1, 1, 2 + a)
+        unit_interleave(("q", 1, 0))
         z_add((0, 2))
-        u_quant((1, 1))
+        unit_quantize(("q", 1, 0))
         z_add((0, 3))
-        stage1((1, 2), 2)
-        stage1((1, 2), 3)
+
+        for t in range(SLOTS):
+            q_slot(1, last, t)
         z_cap((0, 0))
+        unit_interleave(("q", 1, 1))
         z_cap((0, 1))
-        z_mm((1, 0), range(NG - 1))
-        z_mm((1, 1), range(NG - 1))
-        z_mm((1, 2), range(NG - 1), True)
-        z_mm((1, 3), range(NG - 1), True)
-        z_tanh((0, 2))
-        z_tanh((0, 3))
-        u_inter((1, 2))
-        z_round((0, 0), S)
-        z_round((0, 1), S)
-        z_turn((0, 0))
-        z_turn((0, 1))
+        unit_quantize(("q", 1, 1))
+
+        for G in range(last):
+            for a in range(ROW_TILES):
+                z_pass((1, a), G)
+        for a in range(2):
+            z_tanh((0, 2 + a))
+        for a in range(2):
+            y_round((0, a), on_scalar)
+        for a in range(2):
+            y_turn((0, a))
+        unit_interleave(("q", 1, last))
         z_cap((0, 2))
-        u_quant((1, 2))
+        unit_quantize(("q", 1, last))
         z_cap((0, 3))
-        for a in range(NA):
-            z_mm((1, a), range(NG - 1, NG))
-        z_round((0, 2), S)
-        z_evac((0, 0))
-        z_evac((0, 1))
-        z_round((0, 3), S)
-        z_turn((0, 2))
-        z_turn((0, 3))
-        z_add((1, 0))
-        z_add((1, 1))
-        z_evac((0, 2))
-        z_evac((0, 3))
-        z_tanh((1, 0))
-        z_add((1, 2))
-        z_tanh((1, 1))
-        z_add((1, 3))
-        for a in range(NA):
-            z_quant((0, a))
-        store_planes(0)
-        z_cap((1, 0))
-        z_tanh((1, 2))
-        z_cap((1, 1))
-        z_tanh((1, 3))
-        z_round((1, 0), S)
-        z_cap_round((1, 2))
-        z_round((1, 1), S)
-        z_cap_round((1, 3))
-        z_cap((1, 2))
-        z_cap((1, 3))
-        z_turn((1, 0))
-        z_turn((1, 2), True)
-        z_turn((1, 1))
-        z_turn((1, 3), True)
-        for a in (0, 2, 1, 3):
-            z_evac((1, a))
-        for a in (0, 2, 1, 3):
-            z_quant((1, a))
-        store_planes(1)
+        for a in range(ROW_TILES):
+            z_pass((1, a), last)
+        y_round((0, 2), on_scalar)
+        for a in range(2):
+            y_empty((0, a))
+        y_round((0, 3), on_scalar)
+        for a in range(2):
+            y_turn((0, 2 + a))
+
+        for a in range(ROW_TILES):
+            z_add((1, a))
+            z_tanh((1, a))
+        for a in range(ROW_TILES):
+            z_cap((1, a))
+        for a in range(2):
+            y_empty((0, 2 + a))
+        for a in range(ROW_TILES):
+            y_round((1, a), on_scalar if a < SCALAR_ROUNDS else on_vector)
+            y_turn((1, a))
+        for a in range(ROW_TILES):
+            y_quantize((0, a))
+        store_codes(0, 0, H)
+        for a in range(ROW_TILES - 1):
+            y_empty((1, a))
+            y_quantize((1, a))
+        store_codes(1, 0, H - PARTS)
+        y_empty((1, ROW_TILES - 1))
+        y_quantize((1, ROW_TILES - 1))
+        store_codes(1, H - PARTS, H)
+        for Q in range(QUADS):
+            (nc.sync if Q % 2 else nc.scalar).dma_start(
+                out=out_2[:, 4 * Q : 4 * Q + 4, :].bitcast(I32),
+                in_=y_scales[32 * Q : 32 * Q + 4 * COL_GROUPS, :].bitcast(I32),
+            )

@@ -53,7 +53,6 @@ def tile_separable_costmap_inflation_k4_kernel(
             return new(name + "_codes", [PARTS, width], U32), new(name + "_scales", [PARTS, width], U8)
 
         ident = new("ident", [PARTS, PARTS], F32)
-        warm = new("warm", [PARTS, 1], F32)
         vec_raw = new("vec_raw", [PARTS, PASS], BF16)
         vec_sorted = new("vec_sorted", [PARTS, PASS], F32)
         vec = new("vec", [PARTS, SLOTS, 2 * OBJ_GROUPS], F32)
@@ -260,7 +259,6 @@ def tile_separable_costmap_inflation_k4_kernel(
 
 
         nc.vector.memset(u_sc_raw[:].bitcast(I32), 0)
-        nc.vector.memset(warm[:], 0.0)
         nc.vector.memset(v_sc_raw[:].bitcast(I32), 0)
         nc.vector.memset(vec_sorted[:], 0.0)
         make_identity(nc, ident[:])
@@ -284,8 +282,6 @@ def tile_separable_costmap_inflation_k4_kernel(
         load_c(1, 1)
         nc.sync.dma_start(out=static_sb[:], in_=static_map.rearrange("(a p) w -> p a w", p=PARTS))
         nc.sync.dma_start(out=cap_sb[:], in_=cap.partition_broadcast(PARTS))
-
-        nc.scalar.activation(out=warm[:], in_=warm[:], func=ACT.Tanh)
 
         nc.vector.tensor_copy(
             out=r_sorted[:], in_=r_raw[0][:].bitcast(F32).rearrange("p i (m u) -> p i u m", u=2)

from contextlib import ExitStack

import concourse.mybir as mybir
from concourse.masks import make_identity

H, W, J = 512, 1024, 1536
FLOPS = 2 * H * H * J + 2 * W * W * J + 2 * H * W * J

F32 = mybir.dt.float32
BF16 = mybir.dt.bfloat16
U32 = mybir.dt.uint32
I32 = mybir.dt.int32
U8 = mybir.dt.uint8
FP8X4 = mybir.dt.float8_e4m3fn_x4
FP4X4 = mybir.dt.float4_e2m1fn_x4
ACT = mybir.ActivationFunctionType
ALU = mybir.AluOpType

PARTS = 128
SLOTS = 4
PASS = PARTS * SLOTS
BLOCKS = 16
RUN = 8
QUADS = 4
OBJ_GROUPS = J // PASS
COL_GROUPS = W // PASS
ROW_TILES = H // PARTS
ROW_HALF = H // 2
ROTATE = 3

SCALAR_FROM_C00 = 320
SCALAR_FROM_C10 = 384
SCALAR_ROUNDS = 2


def tile_separable_costmap_inflation_k4_kernel(
    tc, row_kernel, col_kernel, u_words, u_scales, v_words, v_scales, strength, base, static_map, cap,
    out_0, out_1, out_2,
):
    nc = tc.nc
    on_vector, on_scalar = nc.vector.tensor_copy, nc.scalar.copy
    with ExitStack() as ctx:
        sb = ctx.enter_context(tc.tile_pool(name="sb", bufs=1))
        ps_mm = ctx.enter_context(tc.psum_pool(name="ps_mm", bufs=4))
        ps_z = ctx.enter_context(tc.psum_pool(name="ps_z", bufs=2))
        ps_tr = ctx.enter_context(tc.psum_pool(name="ps_tr", bufs=2))
        ctx.enter_context(tc.manual_schedule())

        def new(name, shape, dtype):
            return sb.tile(shape, dtype, name=name, align_bytes=64)

        def mx_pair(name, width):
            return new(name + "_codes", [PARTS, width], U32), new(name + "_scales", [PARTS, width], U8)

        ident = new("ident", [PARTS, PARTS], F32)
        vec_raw = new("vec_raw", [PARTS, PASS], BF16)
        vec_sorted = new("vec_sorted", [PARTS, PASS], F32)
        vec = new("vec", [PARTS, SLOTS, 2 * OBJ_GROUPS], F32)
        r_raw = [new("r_raw%d" % b, [PARTS, 2, H], BF16) for b in range(2)]
        r_sorted = new("r_sorted", [PARTS, 2, 2, PARTS], F32)
        r_words = [new("r_words%d" % b, [PARTS, ROW_HALF, SLOTS], BF16) for b in range(2)]
        r_mx = [mx_pair("r%d" % b, ROW_HALF) for b in range(2)]
        u_raw = new("u_raw", [PARTS, 2 * J], U8)
        u_codes = new("u_codes", [PARTS, 2 * J], U8)
        u_sc_raw = new("u_sc_raw", [PARTS, J], U8)
        u_sc = new("u_sc", [PARTS, J], U8)
        v_raw = [new("v_raw%d" % G, [PARTS, COL_GROUPS, PASS], U32) for G in range(OBJ_GROUPS)]
        v_codes = [new("v_codes%d" % G, [PARTS, COL_GROUPS, PASS], U32) for G in range(OBJ_GROUPS)]
        v_sc_raw = new("v_sc_raw", [PARTS, J], U8)
        v_sc = new("v_sc", [PARTS, J], U8)
        c_parts = [(g, half) for g in range(COL_GROUPS) for half in range(COL_GROUPS)]
        c_raw = {c: new("c_raw%d%d" % c, [PARTS, SLOTS, PASS], BF16) for c in c_parts}
        c_words = {c: new("c_words%d%d" % c, [PARTS, PASS, SLOTS], BF16) for c in c_parts}
        c_mx = {c: mx_pair("c%d%d" % c, PASS) for c in c_parts}

        by_slot, by_word, unit_mx = {}, {}, {}
        for kind, width, word_tiles in (("q", PASS, 2), ("p", ROW_HALF, ROTATE)):
            slot_ring = [new("%s_slot%d" % (kind, i), [PARTS, SLOTS, width], BF16) for i in range(ROTATE)]
            word_ring = [new("%s_word%d" % (kind, i), [PARTS, width, SLOTS], BF16) for i in range(word_tiles)]
            for i in range(2 * OBJ_GROUPS):
                unit = (kind, i // OBJ_GROUPS, i % OBJ_GROUPS)
                by_slot[unit] = slot_ring[i % ROTATE]
                by_word[unit] = word_ring[i % word_tiles]
                unit_mx[unit] = mx_pair("%s%d%d" % unit, width)

        static_sb = new("static_sb", [PARTS, ROW_TILES, W], BF16)
        cap_sb = new("cap_sb", [PARTS, W], BF16)
        cells = [(half, a) for half in range(COL_GROUPS) for a in range(ROW_TILES)]
        pre = {c: new("pre%d%d" % c, [PARTS, PASS], F32) for c in cells}
        sat = {c: new("sat%d%d" % c, [PARTS, PASS], F32) for c in cells}
        y = {c: new("y%d%d" % c, [PARTS, PASS], F32) for c in cells}
        y_bf = {c: new("y_bf%d%d" % c, [PARTS, PASS], BF16) for c in cells}
        y_words = {c: new("y_words%d%d" % c, [PARTS, PARTS, SLOTS], BF16) for c in cells}
        y_codes = [new("y_codes%d" % half, [PARTS, H], U32) for half in range(COL_GROUPS)]
        y_scales = new("y_scales", [PARTS, H], U8)
        z_bank, turned = {}, {}

        def load_r(b):
            src = row_kernel[ROW_HALF * b : ROW_HALF * (b + 1), :]
            nc.sync.dma_start(out=r_raw[b][:], in_=src.rearrange("(i p) k -> p i k", p=PARTS))

        def load_c(g, half):
            src = col_kernel[PASS * g : PASS * (g + 1), PASS * half : PASS * (half + 1)]
            nc.sync.dma_start(out=c_raw[g, half][:], in_=src.rearrange("(p t) w -> p t w", t=SLOTS))

        def load_v(G):
            src = v_words.rearrange("g p n t -> p g (n t)")[:, :, SLOTS * PASS * G : SLOTS * PASS * (G + 1)]
            nc.sync.dma_start(out=v_raw[G][:].bitcast(I32), in_=src.bitcast(I32))

        def load_scales(queue, dst, src, quads):
            rows = 4 * src.shape[0]
            for Q in quads:
                queue.dma_start(
                    out=dst[32 * Q : 32 * Q + rows, :].bitcast(I32), in_=src[:, 4 * Q : 4 * Q + 4, :].bitcast(I32)
                )

        def sort_objects(dst, src, run_words):
            nc.vector.tensor_copy(
                out=dst.bitcast(I32).rearrange("p (G t q r) -> p G t q r", t=SLOTS, q=BLOCKS, r=run_words),
                in_=src.bitcast(I32).rearrange("p (G q t r) -> p G t q r", t=SLOTS, q=BLOCKS, r=run_words),
            )

        def sort_v(G):
            sort_objects(v_codes[G][:].rearrange("p g n -> p (g n)"), v_raw[G][:].rearrange("p g n -> p (g n)"), RUN)

        def interleave(copy, words, slots, c0, c1):
            copy(
                out=words[:, c0:c1, :].rearrange("p (c i) t -> p c t i", i=4),
                in_=slots[:, :, c0:c1].rearrange("p t (c i) -> p c t i", i=4),
            )

        def quantize(codes, scales, words):
            nc.vector.quantize_mx(out=codes.bitcast(FP8X4), scales=scales, in_=words.rearrange("p n t -> p (n t)"))

        def c_interleave(copy, g, half, c0, c1):
            interleave(copy, c_words[g, half], c_raw[g, half], c0, c1)

        def c_quantize(g, half):
            quantize(c_mx[g, half][0][:], c_mx[g, half][1][:], c_words[g, half][:])

        def turn_r(b, pairs_of):
            bank = ps_tr.tile([PARTS, 2, 2, PARTS], F32, name="tr")
            for i in range(2):
                for u in range(2):
                    nc.tensor.transpose(bank[:, i, u, :], pairs_of(i, u), ident[:])
            dst = r_words[b][:].rearrange("p n t -> p (n t)").bitcast(F32)
            nc.scalar.copy(
                out=dst.rearrange("p (i n u) -> p i n u", i=2, u=2), in_=bank[:].rearrange("p i u n -> p i n u")
            )

        def r_quantize(b):
            quantize(r_mx[b][0][:], r_mx[b][1][:], r_words[b][:])

        def p_unit(b, G):
            for t0 in range(0, SLOTS, 2):
                bank = ps_mm.tile([PARTS, 2, ROW_HALF], F32, name="mm")
                for e in range(2):
                    c0 = PASS * G + PARTS * (t0 + e)
                    nc.tensor.matmul_mx(
                        out=bank[:, e, :],
                        lhsT=u_codes[:, 2 * c0 : 2 * (c0 + PARTS)].bitcast(FP4X4),
                        lhsT_scale=u_sc[:, c0 : c0 + PARTS],
                        rhs=r_mx[b][0][:].bitcast(FP8X4),
                        rhs_scale=r_mx[b][1][:],
                        start=True,
                        stop=True,
                    )
                for e in range(2):
                    nc.scalar.activation(
                        out=by_slot["p", b, G][:, t0 + e, :], in_=bank[:, e, :], func=ACT.Copy,
                        scale=vec[:, t0 + e, G : G + 1],
                    )

        def q_slot(half, G, t):
            bank = ps_mm.tile([PARTS, PASS], F32, name="mm")
            c0 = PASS * G + PARTS * t
            for g in range(COL_GROUPS):
                nc.tensor.matmul_mx(
                    out=bank[:],
                    lhsT=v_codes[G][:, g, PARTS * t : PARTS * (t + 1)].bitcast(FP8X4),
                    lhsT_scale=v_sc[4 * g :, c0 : c0 + PARTS],
                    rhs=c_mx[g, half][0][:].bitcast(FP8X4),
                    rhs_scale=c_mx[g, half][1][:],
                    start=(g == 0),
                    stop=(g == COL_GROUPS - 1),
                )
            nc.scalar.activation(
                out=by_slot["q", half, G][:, t, :], in_=bank[:], func=ACT.Identity,
                bias=vec[:, t, OBJ_GROUPS + G : OBJ_GROUPS + G + 1],
            )

        def unit_interleave(unit, copy=on_vector):
            interleave(copy, by_word[unit], by_slot[unit], 0, by_word[unit].shape[1])

        def unit_quantize(unit):
            quantize(unit_mx[unit][0][:], unit_mx[unit][1][:], by_word[unit][:])

        def z_pass(c, G):
            half, a = c
            if G == 0:
                spare = half == 1 and a >= 2
                z_bank[c] = (ps_mm if spare else ps_z).tile([PARTS, PASS], F32, name="mm" if spare else "z")
            p_codes, p_scales = unit_mx["p", a // 2, G]
            q_codes, q_scales = unit_mx["q", half, G]
            rows = slice(PARTS * (a % 2), PARTS * (a % 2 + 1))
            nc.tensor.matmul_mx(
                out=z_bank[c][:],
                lhsT=p_codes[:, rows].bitcast(FP8X4),
                lhsT_scale=p_scales[:, rows],
                rhs=q_codes[:].bitcast(FP8X4),
                rhs_scale=q_scales[:],
                start=(G == 0),
                stop=(G == OBJ_GROUPS - 1),
            )

        def z_add(c):
            half, a = c
            nc.vector.tensor_tensor(
                out=pre[c][:], in0=z_bank[c][:], in1=static_sb[:, a, PASS * half : PASS * (half + 1)], op=ALU.add
            )

        def z_tanh(c):
            nc.scalar.activation(out=sat[c][:], in_=pre[c][:], func=ACT.Tanh)

        def z_cap(c):
            half, a = c
            cols = slice(PASS * half, PASS * (half + 1))
            nc.vector.tensor_tensor(out=y[c][:], in0=sat[c][:], in1=cap_sb[:, cols], op=ALU.mult)
            nc.sync.dma_start(out=out_0[PARTS * a : PARTS * (a + 1), cols], in_=y[c][:])

        def y_round(c, copy):
            copy(
                out=y_bf[c][:].rearrange("p (u m e) -> p u m e", u=2, e=2),
                in_=y[c][:].rearrange("p (m u e) -> p u m e", u=2, e=2),
            )

        def y_turn(c):
            half, a = c
            spare = half == 1 and a >= 2
            turned[c] = (ps_mm if spare else ps_tr).tile([PARTS, 2, PARTS], F32, name="mm" if spare else "tr")
            pairs = y_bf[c][:].bitcast(F32)
            for u in range(2):
                nc.tensor.transpose(turned[c][:, u, :], pairs[:, PARTS * u : PARTS * (u + 1)], ident[:])

        def y_empty(c):
            dst = y_words[c][:].rearrange("p n t -> p (n t)").bitcast(F32)
            nc.scalar.copy(out=dst.rearrange("p (n u) -> p n u", u=2), in_=turned[c][:].rearrange("p u n -> p n u"))

        def y_quantize(c):
            half, a = c
            rows = slice(PARTS * a, PARTS * (a + 1))
            quantize(y_codes[half][:, rows], y_scales[4 * half :, rows], y_words[c][:])

        def store_codes(half, m0, m1):
            nc.sync.dma_start(
                out=out_1[half, :, m0:m1, :].rearrange("p m t -> p (m t)").bitcast(I32),
                in_=y_codes[half][:, m0:m1].bitcast(I32),
            )


        nc.vector.memset(u_sc_raw[:].bitcast(I32), 0)
        nc.vector.memset(v_sc_raw[:].bitcast(I32), 0)
        nc.vector.memset(vec_sorted[:], 0.0)
        make_identity(nc, ident[:])

        load_r(0)
        nc.sync.dma_start(out=u_raw[:].bitcast(I32), in_=u_words[0].bitcast(I32))
        load_c(0, 0)
        for i, vector in enumerate((strength, base)):
            nc.scalar.dma_start(
                out=vec_raw[OBJ_GROUPS * i : OBJ_GROUPS * (i + 1), :], in_=vector.rearrange("(G n) -> G n", G=OBJ_GROUPS)
            )
        load_scales(nc.scalar, u_sc_raw, u_scales, range(QUADS - 1))
        load_scales(nc.sync, u_sc_raw, u_scales, range(QUADS - 1, QUADS))
        load_c(1, 0)
        load_v(0)
        load_scales(nc.sync, v_sc_raw, v_scales, range(QUADS))
        load_r(1)
        load_v(1)
        load_c(0, 1)
        load_v(2)
        load_c(1, 1)
        nc.sync.dma_start(out=static_sb[:], in_=static_map.rearrange("(a p) w -> p a w", p=PARTS))
        nc.sync.dma_start(out=cap_sb[:], in_=cap.partition_broadcast(PARTS))

        nc.vector.tensor_copy(
            out=r_sorted[:], in_=r_raw[0][:].bitcast(F32).rearrange("p i (m u) -> p i u m", u=2)
        )
        turn_r(0, lambda i, u: r_sorted[:, i, u, :])
        sort_objects(u_codes[:], u_raw[:], RUN // 2)
        nc.vector.tensor_copy(
            out=vec_sorted[0 : 2 * OBJ_GROUPS, :].rearrange("p (t q r) -> p t q r", t=SLOTS, q=BLOCKS),
            in_=vec_raw[0 : 2 * OBJ_GROUPS, :].rearrange("p (q t r) -> p t q r", t=SLOTS, q=BLOCKS),
        )
        c_interleave(on_vector, 0, 0, 0, PARTS)
        r_quantize(0)
        sort_objects(u_sc[:], u_sc_raw[:], RUN // 4)
        c_interleave(on_scalar, 0, 0, SCALAR_FROM_C00, PASS)
        vec_bank = ps_z.tile([PARTS, SLOTS, PARTS], F32, name="z")
        for t in range(SLOTS):
            nc.tensor.transpose(vec_bank[:, t, :], vec_sorted[:, PARTS * t : PARTS * (t + 1)], ident[:])
        nc.scalar.copy(out=vec[:], in_=vec_bank[:, :, 0 : 2 * OBJ_GROUPS])
        c_interleave(on_vector, 0, 0, PARTS, SCALAR_FROM_C00)
        c_interleave(on_scalar, 1, 0, SCALAR_FROM_C10, PASS)

        for G in range(OBJ_GROUPS):
            p_unit(0, G)
        c_interleave(on_vector, 1, 0, 0, SCALAR_FROM_C10)
        c_quantize(0, 0)
        sort_v(0)
        c_quantize(1, 0)
        sort_objects(v_sc[:], v_sc_raw[:], RUN // 4)

        between = [
            [lambda: sort_v(1)],
            [lambda: c_interleave(on_vector, 0, 1, 0, PASS), lambda: sort_v(2)],
            [lambda: r_quantize(1)],
        ]
        for G in range(OBJ_GROUPS):
            for t in range(SLOTS):
                q_slot(0, G, t)
                if (G, t) == (0, 1):
                    turn_r(1, lambda i, u: r_raw[1][:, i, :].bitcast(F32)[:, u : 2 * PARTS : 2])
            unit_interleave(("p", 0, G))
            for work in between[G]:
                work()
            unit_quantize(("p", 0, G))

        between = [
            lambda: c_quantize(0, 1),
            lambda: c_interleave(on_vector, 1, 1, 0, PASS),
            lambda: c_quantize(1, 1),
        ]
        for G in range(OBJ_GROUPS):
            p_unit(1, G)
            unit_interleave(("q", 0, G))
            between[G]()
            unit_quantize(("q", 0, G))
        last = OBJ_GROUPS - 1
        unit_interleave(("p", 1, last), on_scalar)

        for a in range(2):
            for G in range(last):
                z_pass((0, a), G)
        for t in range(SLOTS - 1):
            q_slot(1, 0, t)
        for a in range(2):
            z_pass((0, a), last)
        q_slot(1, 0, SLOTS - 1)
        for G in range(last):
            unit_interleave(("p", 1, G))
        for G in range(OBJ_GROUPS):
            unit_quantize(("p", 1, G))
        for a in range(2):
            z_add((0, a))

        for t in range(2):
            q_slot(1, 1, t)
        for a in range(2):
            for G in range(OBJ_GROUPS):
                z_pass((0, 2 + a), G)
            z_tanh((0, a))
            q_slot(1, 1, 2 + a)
        unit_interleave(("q", 1, 0))
        z_add((0, 2))
        unit_quantize(("q", 1, 0))
        z_add((0, 3))

        for t in range(SLOTS):
            q_slot(1, last, t)
        z_cap((0, 0))
        unit_interleave(("q", 1, 1))
        z_cap((0, 1))
        unit_quantize(("q", 1, 1))

        for G in range(last):
            for a in range(ROW_TILES):
                z_pass((1, a), G)
        for a in range(2):
            z_tanh((0, 2 + a))
        for a in range(2):
            y_round((0, a), on_scalar)
        for a in range(2):
            y_turn((0, a))
        unit_interleave(("q", 1, last))
        z_cap((0, 2))
        unit_quantize(("q", 1, last))
        z_cap((0, 3))
        for a in range(ROW_TILES):
            z_pass((1, a), last)
        y_round((0, 2), on_scalar)
        for a in range(2):
            y_empty((0, a))
        y_round((0, 3), on_scalar)
        for a in range(2):
            y_turn((0, 2 + a))

        for a in range(ROW_TILES):
            z_add((1, a))
            z_tanh((1, a))
        for a in range(ROW_TILES):
            z_cap((1, a))
        for a in range(2):
            y_empty((0, 2 + a))
        for a in range(ROW_TILES):
            y_round((1, a), on_scalar if a < SCALAR_ROUNDS else on_vector)
            y_turn((1, a))
        for a in range(ROW_TILES):
            y_quantize((0, a))
        store_codes(0, 0, H)
        for a in range(ROW_TILES - 1):
            y_empty((1, a))
            y_quantize((1, a))
        store_codes(1, 0, H - PARTS)
        y_empty((1, ROW_TILES - 1))
        y_quantize((1, ROW_TILES - 1))
        store_codes(1, H - PARTS, H)
        for Q in range(QUADS):
            (nc.sync if Q % 2 else nc.scalar).dma_start(
                out=out_2[:, 4 * Q : 4 * Q + 4, :].bitcast(I32),
                in_=y_scales[32 * Q : 32 * Q + 4 * COL_GROUPS, :].bitcast(I32),
            )
